import numpy as np
import ml_dtypes


def mxq(x, axis, fmt="e4m3"):
    dtype, down = {"e4m3": (ml_dtypes.float8_e4m3fn, 7), "e5m2": (ml_dtypes.float8_e5m2, 14)}[fmt]
    v = np.moveaxis(np.asarray(x, np.float32).astype(ml_dtypes.bfloat16).astype(np.float64), axis, -1)
    blocks = v.reshape(v.shape[:-1] + (-1, 32))
    amax = np.abs(blocks).max(-1, keepdims=True)
    byte = np.maximum(np.where(amax > 0, np.frexp(amax)[1] - 1 + 127, 0) - down, 1)
    scale = np.exp2(byte - 127.0)
    codes = (blocks / scale).astype(np.float32).astype(dtype).astype(np.float64)
    return np.moveaxis((codes * scale).reshape(v.shape), -1, axis)


WIDE = False


def mx_kscale(k):
    if not WIDE:
        return np.ones(k)
    levels = np.array([10, -10, 5, -5, 0])
    if k % 512:
        return np.exp2(np.random.permutation(np.resize(levels, k // 32))).repeat(32)
    a = np.empty((k // 512, 16))
    for p in range(k // 512):
        a[p, :8] = np.random.permutation(np.resize(levels, 8))
        for g in range(8):
            far = levels[np.abs(levels - a[p, g]) >= 10]
            a[p, g + 8] = far[np.random.randint(len(far))]
    return np.exp2(a.ravel()).repeat(32)


def f64(x):
    return np.asarray(x).astype(np.float64)


def striped(idx):
    return np.tile(idx.reshape(-1, 16).T, (8, 1)).astype(np.uint16)


def unstriped(offs):
    return offs[:16].T.reshape(-1).astype(np.int64)


E2M1 = np.array([0.0, 0.5, 1.0, 1.5, 2.0, 3.0, 4.0, 6.0, -0.0, -0.5, -1.0, -1.5, -2.0, -3.0, -4.0, -6.0])


def pack_weight(w, fmt):
    k, n = w.shape
    w = f64(np.asarray(w, np.float32).astype(ml_dtypes.bfloat16)).reshape(k // 32, 32, n)
    amax = np.abs(w).max(1)
    if fmt == "e4m3":
        byte = np.frexp(amax)[1] - 1 + 127 - 7
    else:
        mant, ex = np.frexp(amax / 6.0)
        byte = np.where(mant > 0.5, ex, ex - 1) + 127
    byte = np.clip(np.where(amax > 0, byte, 1), 1, 254)
    scaled = (w * np.exp2(127.0 - byte)[:, None, :]).reshape(k, n).astype(np.float32)
    by_word = np.ascontiguousarray(scaled.reshape(k // 512, 128, 4, n).transpose(0, 1, 3, 2))
    if fmt == "e4m3":
        words = by_word.astype(ml_dtypes.float8_e4m3fn).view(np.uint8)
    else:
        c = by_word.astype(ml_dtypes.float4_e2m1fn).view(np.uint8) & 0xF
        words = (c[..., 0::2] | (c[..., 1::2] << 4)).reshape(k // 512, 128, 2 * n)
    return np.ascontiguousarray(words), np.ascontiguousarray(byte.astype(np.uint8).reshape(k // 512, 16, n))


def unpack_weight(words, scales, fmt):
    g, _, n = scales.shape
    words = np.ascontiguousarray(words).reshape(g, 128, n, -1)
    if fmt == "e4m3":
        vals = words.view(ml_dtypes.float8_e4m3fn).astype(np.float64)
    else:
        nib = np.empty((g, 128, n, 4), np.uint8)
        nib[..., 0::2] = words & 0xF
        nib[..., 1::2] = words >> 4
        vals = E2M1[nib]
    vals = vals * np.repeat(np.exp2(scales.astype(np.float64) - 127.0), 8, axis=1)[..., None]
    return vals.transpose(0, 1, 3, 2).reshape(g * 512, n)


def pack_table(v):
    words, scales = pack_weight(v, "e4m3")
    return np.concatenate([words.reshape(words.shape[0], -1), scales.reshape(scales.shape[0], -1)], axis=1)


def unpack_table(tab):
    g, t = tab.shape[0], tab.shape[1] // 528
    return unpack_weight(tab[:, :512 * t].reshape(g, 128, t, 4), tab[:, 512 * t:].reshape(g, 16, t), "e4m3")


K, L, M, T, S = 1536, 512, 128, 1024, 512


def setup_inputs():
    n = np.random.standard_normal
    s1 = mx_kscale(K)[:, None]
    s2 = mx_kscale(L)[:, None]
    p_w4 = pack_weight(n((K, M)) / np.sqrt(K) / s1, "e2m1")
    return {
        "tab": pack_table(n((K, T)) * s1),
        "w4_words": p_w4[0],
        "w4_scales": p_w4[1],
        "x": (n((L, S)) * s2).astype(np.float32),
        "u": (n((L, M)) / np.sqrt(L) / s2).astype(np.float32),
        "offs": striped(np.random.permutation(T)[:S]),
    }


def reference(tab, w4_words, w4_scales, x, u, offs):
    tab_ = unpack_table(tab)[:, unstriped(offs)]
    w4_ = unpack_weight(w4_words, w4_scales, "e2m1")
    x_ = mxq(f64(x), 0, "e4m3")
    u_ = mxq(f64(u), 0, "e4m3")
    y = tab_.T @ w4_ + x_.T @ u_
    return y

@@ -1,0 +1,168 @@
+import concourse.mybir as mybir
+
+K, L, M, T, S = 1536, 512, 128, 1024, 512
+FLOPS = 2 * S * M * (K + L)
+
+F32 = mybir.dt.float32
+BF16 = mybir.dt.bfloat16
+I32 = mybir.dt.int32
+U32 = mybir.dt.uint32
+U16 = mybir.dt.uint16
+U8 = mybir.dt.uint8
+E4M3 = mybir.dt.float8_e4m3fn_x4
+E2M1 = mybir.dt.float4_e2m1fn_x4
+
+P = 128
+PASSES = K // 512
+HALF = S // 2
+TILES = S // P
+
+
+def tile_list_tabx_tm_none_kernel(tc, tab, w4_words, w4_scales, x, u, offs, out):
+    nc = tc.nc
+    with (
+        tc.tile_pool(name="keep", bufs=1) as keep,
+        tc.psum_pool(name="psum", bufs=1) as psum,
+    ):
+        offsets = keep.tile([P, S // 16], U16, name="offsets")
+        nc.sync.dma_start(offsets[:], offs)
+
+        scales01 = keep.tile([P, T // 4], I32, name="scales01", align_bytes=64)
+        nc.gpsimd.memset(scales01[:], 0)
+        scales2 = keep.tile([P, T // 4], I32, name="scales2", align_bytes=64)
+        w_scales = keep.tile([P, PASSES, M], U8, name="w_scales", align_bytes=64)
+        nc.gpsimd.memset(w_scales[:].bitcast(I32), 0)
+        warm = keep.tile([P, 1], F32, name="warm")
+        warmed = keep.tile([P, 1], F32, name="warmed")
+        nc.vector.memset(warm[:], 0.0)
+        picked = [keep.tile([P, S], U8, name="picked%d" % a, align_bytes=64) for a in range(PASSES)]
+        nc.vector.memset(scales2[:], 0)
+        nc.vector.memset(picked[1][:].bitcast(I32), 0)
+
+        def load_words(a):
+            words = keep.tile([P, T], I32, name="tab_words%d" % a, align_bytes=64)
+            nc.sync.dma_start(words[:], tab[a, 0 : 512 * T].rearrange("(p c) -> p c", p=P).bitcast(I32))
+            return words
+
+        x_rows = x.rearrange("(p j) s -> p j s", j=4)
+
+        def load_x(h):
+            raw = keep.tile([P, 4, HALF], F32, name="x_raw%d" % h)
+            nc.sync.dma_start(raw[:], x_rows[:, :, h * HALF : (h + 1) * HALF])
+            return raw
+
+        scale_rows = tab[:, 512 * T :].rearrange("a (q t) -> a q t", t=T)
+        for quad in range(4):
+            nc.sync.dma_start(
+                scales01[32 * quad : 32 * quad + 8, :],
+                scale_rows[0:2, 4 * quad : 4 * quad + 4, :].bitcast(I32),
+            )
+        nc.scalar.copy(warmed[:], warm[:])
+        tab_words = [load_words(0)]
+        x_raw = [load_x(0)]
+        u_raw = keep.tile([P, 4, M], F32, name="u_raw")
+        nc.sync.dma_start(u_raw[:], u.rearrange("(p j) n -> p j n", j=4))
+        for quad in range(4):
+            nc.scalar.dma_start(
+                scales2[32 * quad : 32 * quad + 4, :],
+                scale_rows[2, 4 * quad : 4 * quad + 4, :].bitcast(I32),
+            )
+        tab_words.append(load_words(1))
+        tab_words.append(load_words(2))
+        w_codes = keep.tile([P, PASSES, 2 * M], U8, name="w_codes", align_bytes=64)
+        nc.sync.dma_start(w_codes[:].bitcast(I32), w4_words.rearrange("a p c -> p a c").bitcast(I32))
+        w_scale_rows = w4_scales.rearrange("a q n -> q a n")
+        for quad, queue in enumerate((nc.gpsimd, nc.gpsimd, nc.sync, nc.sync)):
+            queue.dma_start(
+                w_scales[32 * quad : 32 * quad + 4, :, :].bitcast(I32),
+                w_scale_rows[4 * quad : 4 * quad + 4, :, :].bitcast(I32),
+            )
+        x_raw.append(load_x(1))
+
+        x_bf = [keep.tile([P, HALF, 4], BF16, name="x_bf0", align_bytes=64)]
+        u_bf = keep.tile([P, M, 4], BF16, name="u_bf", align_bytes=64)
+        nc.scalar.copy(x_bf[0][:], x_raw[0][:].rearrange("p j s -> p s j"))
+        nc.scalar.copy(u_bf[:], u_raw[:].rearrange("p j n -> p n j"))
+        x_bf += [keep.tile([P, P, 4], BF16, name="x_bf%d" % h, align_bytes=64) for h in range(1, 3)]
+        nc.scalar.copy(x_bf[1][:], x_raw[1][:, :, 0:P].rearrange("p j s -> p s j"))
+
+        u_codes = keep.tile([P, M], U32, name="u_codes", align_bytes=64)
+        u_scales = keep.tile([P, M], U8, name="u_scales", align_bytes=64)
+        x_codes = keep.tile([P, S], U32, name="x_codes", align_bytes=64)
+        x_scales = keep.tile([P, S], U8, name="x_scales", align_bytes=64)
+        picked_words = [
+            keep.tile([P, S], U32, name="picked_words%d" % a, align_bytes=64) for a in range(PASSES)
+        ]
+        acc = [psum.tile([P, M], F32, name="acc%d" % c) for c in range(TILES)]
+
+        def gather_words(a, c0, c1):
+            nc.vector.tensor_copy(
+                picked_words[a][:, c0:c1],
+                tab_words[a][:].bitcast(U32).indirect(offsets[:, c0 // 16 : c1 // 16]),
+            )
+
+        def quantize_x(bf, c0, c1):
+            cols = slice(c0, c1)
+            nc.vector.quantize_mx(
+                x_codes[:, cols].bitcast(E4M3), x_scales[:, cols], bf[:].rearrange("p s j -> p (s j)")
+            )
+
+        def dense_pass(c):
+            cols = slice(c * P, (c + 1) * P)
+            nc.tensor.matmul_mx(
+                out=acc[c][:],
+                lhsT=x_codes[:, cols].bitcast(E4M3),
+                lhsT_scale=x_scales[:, cols],
+                rhs=u_codes[:].bitcast(E4M3),
+                rhs_scale=u_scales[:],
+                start=False,
+                stop=(c >= TILES // 2),
+            )
+
+        def table_pass(a, c):
+            cols = slice(c * P, (c + 1) * P)
+            nc.tensor.matmul_mx(
+                out=acc[c][:],
+                lhsT=picked_words[a][:, cols].bitcast(E4M3),
+                lhsT_scale=picked[a][:, cols],
+                rhs=w_codes[:, a, :].bitcast(E2M1),
+                rhs_scale=w_scales[:, a, :],
+                start=(a == 0),
+                stop=(a == PASSES - 1 and c < TILES // 2),
+            )
+
+        nc.vector.tensor_copy(picked[0][:], scales01[:].bitcast(U8).indirect(offsets[:]))
+        gather_words(0, 0, S)
+        for quad in range(4):
+            nc.sync.dma_start(
+                picked[1][32 * quad : 32 * quad + 4, :].bitcast(I32),
+                picked[0][32 * quad + 4 : 32 * quad + 8, :].bitcast(I32),
+            )
+        nc.vector.tensor_copy(picked[2][:], scales2[:].bitcast(U8).indirect(offsets[:]))
+        gather_words(1, 0, S)
+        for c in range(TILES):
+            table_pass(0, c)
+        quantize_x(x_bf[0], 0, HALF)
+        nc.vector.quantize_mx(u_codes[:].bitcast(E4M3), u_scales[:], u_bf[:].rearrange("p n j -> p (n j)"))
+        for c in range(TILES // 2):
+            dense_pass(c)
+        for c in range(TILES):
+            table_pass(1, c)
+
+        def finish(c, copy):
+            result = keep.tile([P, M], F32, name="result%d" % c)
+            copy(result[:], acc[c][:])
+            nc.sync.dma_start(out[c * P : (c + 1) * P, :], result[:])
+
+        gather_words(PASSES - 1, 0, HALF)
+        for c in range(TILES // 2):
+            table_pass(PASSES - 1, c)
+            finish(c, nc.scalar.copy)
+        gather_words(PASSES - 1, HALF, S)
+        for c in range(TILES // 2, TILES):
+            table_pass(PASSES - 1, c)
+        nc.vector.tensor_copy(x_bf[2][:], x_raw[1][:, :, P:HALF].rearrange("p j s -> p s j"))
+        for c, copy in ((2, nc.scalar.copy), (3, nc.vector.tensor_copy)):
+            quantize_x(x_bf[c - 1], c * P, (c + 1) * P)
+            dense_pass(c)
+            finish(c, copy)

@@ -14,7 +14,7 @@ E2M1 = mybir.dt.float4_e2m1fn_x4
 
 P = 128
 PASSES = K // 512
-HALF = S // 2
+SLOTS = 4
 TILES = S // P
 
 
@@ -27,17 +27,27 @@ def tile_list_tabx_tm_none_kernel(tc, tab, w4_words, w4_scales, x, u, offs, out)
         offsets = keep.tile([P, S // 16], U16, name="offsets")
         nc.sync.dma_start(offsets[:], offs)
 
-        scales01 = keep.tile([P, T // 4], I32, name="scales01", align_bytes=64)
-        nc.gpsimd.memset(scales01[:], 0)
-        scales2 = keep.tile([P, T // 4], I32, name="scales2", align_bytes=64)
+        window = keep.tile([P, T // 4], I32, name="window", align_bytes=64)
+        nc.gpsimd.memset(window[:], 0)
         w_scales = keep.tile([P, PASSES, M], U8, name="w_scales", align_bytes=64)
-        nc.gpsimd.memset(w_scales[:].bitcast(I32), 0)
+        nc.vector.memset(w_scales[:].bitcast(I32), 0)
         warm = keep.tile([P, 1], F32, name="warm")
         warmed = keep.tile([P, 1], F32, name="warmed")
         nc.vector.memset(warm[:], 0.0)
-        picked = [keep.tile([P, S], U8, name="picked%d" % a, align_bytes=64) for a in range(PASSES)]
-        nc.vector.memset(scales2[:], 0)
-        nc.vector.memset(picked[1][:].bitcast(I32), 0)
+        planes = keep.tile([P, SLOTS * S], U8, name="planes", align_bytes=64)
+        nc.vector.memset(planes[:].bitcast(I32), 0)
+        nc.scalar.copy(warmed[:], warm[:])
+
+        scale_rows = tab[:, 512 * T :].rearrange("a (q t) -> a q t", t=T)
+        for a in range(PASSES):
+            nc.sync.dma_start(window[a : 16 * SLOTS : SLOTS, :], scale_rows[a].bitcast(I32))
+
+        w_scale_rows = w4_scales.rearrange("a q n -> q a n")
+        for quad in range(4):
+            nc.gpsimd.dma_start(
+                w_scales[32 * quad : 32 * quad + 4, :, :].bitcast(I32),
+                w_scale_rows[4 * quad : 4 * quad + 4, :, :].bitcast(I32),
+            )
 
         def load_words(a):
             words = keep.tile([P, T], I32, name="tab_words%d" % a, align_bytes=64)
@@ -46,46 +56,32 @@ def tile_list_tabx_tm_none_kernel(tc, tab, w4_words, w4_scales, x, u, offs, out)
 
         x_rows = x.rearrange("(p j) s -> p j s", j=4)
 
-        def load_x(h):
-            raw = keep.tile([P, 4, HALF], F32, name="x_raw%d" % h)
-            nc.sync.dma_start(raw[:], x_rows[:, :, h * HALF : (h + 1) * HALF])
+        def load_x(c0, c1):
+            raw = keep.tile([P, 4, c1 - c0], F32, name="x_raw%d" % c0)
+            nc.sync.dma_start(raw[:], x_rows[:, :, c0:c1])
             return raw
 
-        scale_rows = tab[:, 512 * T :].rearrange("a (q t) -> a q t", t=T)
-        for quad in range(4):
-            nc.sync.dma_start(
-                scales01[32 * quad : 32 * quad + 8, :],
-                scale_rows[0:2, 4 * quad : 4 * quad + 4, :].bitcast(I32),
-            )
-        nc.scalar.copy(warmed[:], warm[:])
         tab_words = [load_words(0)]
-        x_raw = [load_x(0)]
         u_raw = keep.tile([P, 4, M], F32, name="u_raw")
         nc.sync.dma_start(u_raw[:], u.rearrange("(p j) n -> p j n", j=4))
-        for quad in range(4):
-            nc.scalar.dma_start(
-                scales2[32 * quad : 32 * quad + 4, :],
-                scale_rows[2, 4 * quad : 4 * quad + 4, :].bitcast(I32),
-            )
         tab_words.append(load_words(1))
         tab_words.append(load_words(2))
+
+        picked = keep.tile([P, S], U8, name="picked", align_bytes=64)
+        nc.vector.tensor_copy(picked[:], window[:].bitcast(U8).indirect(offsets[:]))
+        for quad in range(4):
+            nc.scalar.dma_start(
+                planes[32 * quad : 32 * quad + 4, :].bitcast(I32),
+                picked[16 * quad : 16 * quad + 16, :].bitcast(I32),
+            )
+
         w_codes = keep.tile([P, PASSES, 2 * M], U8, name="w_codes", align_bytes=64)
         nc.sync.dma_start(w_codes[:].bitcast(I32), w4_words.rearrange("a p c -> p a c").bitcast(I32))
-        w_scale_rows = w4_scales.rearrange("a q n -> q a n")
-        for quad, queue in enumerate((nc.gpsimd, nc.gpsimd, nc.sync, nc.sync)):
-            queue.dma_start(
-                w_scales[32 * quad : 32 * quad + 4, :, :].bitcast(I32),
-                w_scale_rows[4 * quad : 4 * quad + 4, :, :].bitcast(I32),
-            )
-        x_raw.append(load_x(1))
+        x_first = load_x(0, 2 * P)
+        x_raw = [x_first[:, :, 0:P], x_first[:, :, P : 2 * P], load_x(2 * P, 3 * P)[:], load_x(3 * P, 4 * P)[:]]
 
-        x_bf = [keep.tile([P, HALF, 4], BF16, name="x_bf0", align_bytes=64)]
         u_bf = keep.tile([P, M, 4], BF16, name="u_bf", align_bytes=64)
-        nc.scalar.copy(x_bf[0][:], x_raw[0][:].rearrange("p j s -> p s j"))
         nc.scalar.copy(u_bf[:], u_raw[:].rearrange("p j n -> p n j"))
-        x_bf += [keep.tile([P, P, 4], BF16, name="x_bf%d" % h, align_bytes=64) for h in range(1, 3)]
-        nc.scalar.copy(x_bf[1][:], x_raw[1][:, :, 0:P].rearrange("p j s -> p s j"))
-
         u_codes = keep.tile([P, M], U32, name="u_codes", align_bytes=64)
         u_scales = keep.tile([P, M], U8, name="u_scales", align_bytes=64)
         x_codes = keep.tile([P, S], U32, name="x_codes", align_bytes=64)
@@ -95,20 +91,35 @@ def tile_list_tabx_tm_none_kernel(tc, tab, w4_words, w4_scales, x, u, offs, out)
         ]
         acc = [psum.tile([P, M], F32, name="acc%d" % c) for c in range(TILES)]
 
-        def gather_words(a, c0, c1):
-            nc.vector.tensor_copy(
-                picked_words[a][:, c0:c1],
-                tab_words[a][:].bitcast(U32).indirect(offsets[:, c0 // 16 : c1 // 16]),
-            )
+        def table_pass(a):
+            nc.vector.tensor_copy(picked_words[a][:], tab_words[a][:].bitcast(U32).indirect(offsets[:]))
+            for c in range(TILES):
+                nc.tensor.matmul_mx(
+                    out=acc[c][:],
+                    lhsT=picked_words[a][:, c * P : (c + 1) * P].bitcast(E4M3),
+                    lhsT_scale=planes[:, a * S + c * P : a * S + (c + 1) * P],
+                    rhs=w_codes[:, a, :].bitcast(E2M1),
+                    rhs_scale=w_scales[:, a, :],
+                    start=(a == 0),
+                    stop=False,
+                )
 
-        def quantize_x(bf, c0, c1):
-            cols = slice(c0, c1)
-            nc.vector.quantize_mx(
-                x_codes[:, cols].bitcast(E4M3), x_scales[:, cols], bf[:].rearrange("p s j -> p (s j)")
-            )
+        table_pass(0)
+        nc.vector.quantize_mx(u_codes[:].bitcast(E4M3), u_scales[:], u_bf[:].rearrange("p n j -> p (n j)"))
+        table_pass(1)
+        table_pass(2)
 
-        def dense_pass(c):
+        rounders = (nc.scalar.copy, nc.vector.tensor_copy, nc.scalar.copy, nc.vector.tensor_copy)
+        emptiers = (nc.scalar.copy, nc.scalar.copy, nc.scalar.copy, nc.vector.tensor_copy)
+        x_bf = []
+        for c in range(TILES):
+            x_bf.append(keep.tile([P, P, 4], BF16, name="x_bf%d" % c, align_bytes=64))
+            rounders[c](x_bf[c][:], x_raw[c].rearrange("p j s -> p s j"))
+        for c in range(TILES):
             cols = slice(c * P, (c + 1) * P)
+            nc.vector.quantize_mx(
+                x_codes[:, cols].bitcast(E4M3), x_scales[:, cols], x_bf[c][:].rearrange("p s j -> p (s j)")
+            )
             nc.tensor.matmul_mx(
                 out=acc[c][:],
                 lhsT=x_codes[:, cols].bitcast(E4M3),
@@ -116,53 +127,8 @@ def tile_list_tabx_tm_none_kernel(tc, tab, w4_words, w4_scales, x, u, offs, out)
                 rhs=u_codes[:].bitcast(E4M3),
                 rhs_scale=u_scales[:],
                 start=False,
-                stop=(c >= TILES // 2),
+                stop=True,
             )
-
-        def table_pass(a, c):
-            cols = slice(c * P, (c + 1) * P)
-            nc.tensor.matmul_mx(
-                out=acc[c][:],
-                lhsT=picked_words[a][:, cols].bitcast(E4M3),
-                lhsT_scale=picked[a][:, cols],
-                rhs=w_codes[:, a, :].bitcast(E2M1),
-                rhs_scale=w_scales[:, a, :],
-                start=(a == 0),
-                stop=(a == PASSES - 1 and c < TILES // 2),
-            )
-
-        nc.vector.tensor_copy(picked[0][:], scales01[:].bitcast(U8).indirect(offsets[:]))
-        gather_words(0, 0, S)
-        for quad in range(4):
-            nc.sync.dma_start(
-                picked[1][32 * quad : 32 * quad + 4, :].bitcast(I32),
-                picked[0][32 * quad + 4 : 32 * quad + 8, :].bitcast(I32),
-            )
-        nc.vector.tensor_copy(picked[2][:], scales2[:].bitcast(U8).indirect(offsets[:]))
-        gather_words(1, 0, S)
-        for c in range(TILES):
-            table_pass(0, c)
-        quantize_x(x_bf[0], 0, HALF)
-        nc.vector.quantize_mx(u_codes[:].bitcast(E4M3), u_scales[:], u_bf[:].rearrange("p n j -> p (n j)"))
-        for c in range(TILES // 2):
-            dense_pass(c)
-        for c in range(TILES):
-            table_pass(1, c)
-
-        def finish(c, copy):
             result = keep.tile([P, M], F32, name="result%d" % c)
-            copy(result[:], acc[c][:])
+            emptiers[c](result[:], acc[c][:])
             nc.sync.dma_start(out[c * P : (c + 1) * P, :], result[:])
-
-        gather_words(PASSES - 1, 0, HALF)
-        for c in range(TILES // 2):
-            table_pass(PASSES - 1, c)
-            finish(c, nc.scalar.copy)
-        gather_words(PASSES - 1, HALF, S)
-        for c in range(TILES // 2, TILES):
-            table_pass(PASSES - 1, c)
-        nc.vector.tensor_copy(x_bf[2][:], x_raw[1][:, :, P:HALF].rearrange("p j s -> p s j"))
-        for c, copy in ((2, nc.scalar.copy), (3, nc.vector.tensor_copy)):
-            quantize_x(x_bf[c - 1], c * P, (c + 1) * P)
-            dense_pass(c)
-            finish(c, copy)

@@ -30,24 +30,24 @@ def tile_list_tabx_tm_none_kernel(tc, tab, w4_words, w4_scales, x, u, offs, out)
         window = keep.tile([P, T // 4], I32, name="window", align_bytes=64)
         nc.gpsimd.memset(window[:], 0)
         w_scales = keep.tile([P, PASSES, M], U8, name="w_scales", align_bytes=64)
-        nc.vector.memset(w_scales[:].bitcast(I32), 0)
+        nc.gpsimd.memset(w_scales[:].bitcast(I32), 0)
         warm = keep.tile([P, 1], F32, name="warm")
         warmed = keep.tile([P, 1], F32, name="warmed")
         nc.vector.memset(warm[:], 0.0)
         planes = keep.tile([P, SLOTS * S], U8, name="planes", align_bytes=64)
         nc.vector.memset(planes[:].bitcast(I32), 0)
-        nc.scalar.copy(warmed[:], warm[:])
 
         scale_rows = tab[:, 512 * T :].rearrange("a (q t) -> a q t", t=T)
         for a in range(PASSES):
             nc.sync.dma_start(window[a : 16 * SLOTS : SLOTS, :], scale_rows[a].bitcast(I32))
 
         w_scale_rows = w4_scales.rearrange("a q n -> q a n")
-        for quad in range(4):
-            nc.gpsimd.dma_start(
+        for quad, queue in enumerate((nc.gpsimd, nc.gpsimd, nc.scalar, nc.scalar)):
+            queue.dma_start(
                 w_scales[32 * quad : 32 * quad + 4, :, :].bitcast(I32),
                 w_scale_rows[4 * quad : 4 * quad + 4, :, :].bitcast(I32),
             )
+        nc.scalar.copy(warmed[:], warm[:])
 
         def load_words(a):
             words = keep.tile([P, T], I32, name="tab_words%d" % a, align_bytes=64)
@@ -70,7 +70,7 @@ def tile_list_tabx_tm_none_kernel(tc, tab, w4_words, w4_scales, x, u, offs, out)
         picked = keep.tile([P, S], U8, name="picked", align_bytes=64)
         nc.vector.tensor_copy(picked[:], window[:].bitcast(U8).indirect(offsets[:]))
         for quad in range(4):
-            nc.scalar.dma_start(
+            nc.sync.dma_start(
                 planes[32 * quad : 32 * quad + 4, :].bitcast(I32),
                 picked[16 * quad : 16 * quad + 16, :].bitcast(I32),
             )

@@ -15,6 +15,7 @@ E2M1 = mybir.dt.float4_e2m1fn_x4
 P = 128
 PASSES = K // 512
 SLOTS = 4
+SLOT_OF_PASS = (0, 2, 1)
 TILES = S // P
 
 
@@ -33,16 +34,16 @@ def tile_list_tabx_tm_none_kernel(tc, tab, w4_words, w4_scales, x, u, offs, out)
         nc.gpsimd.memset(w_scales[:].bitcast(I32), 0)
         warm = keep.tile([P, 1], F32, name="warm")
         warmed = keep.tile([P, 1], F32, name="warmed")
-        nc.vector.memset(warm[:], 0.0)
+        nc.gpsimd.memset(warm[:], 0.0)
         planes = keep.tile([P, SLOTS * S], U8, name="planes", align_bytes=64)
         nc.vector.memset(planes[:].bitcast(I32), 0)
 
         scale_rows = tab[:, 512 * T :].rearrange("a (q t) -> a q t", t=T)
-        for a in range(PASSES):
-            nc.sync.dma_start(window[a : 16 * SLOTS : SLOTS, :], scale_rows[a].bitcast(I32))
+        nc.sync.dma_start(window[0:64:2, :], scale_rows[0:2].rearrange("a q t -> q a t").bitcast(I32))
+        nc.sync.dma_start(window[1:64:4, :], scale_rows[2].bitcast(I32))
 
         w_scale_rows = w4_scales.rearrange("a q n -> q a n")
-        for quad, queue in enumerate((nc.gpsimd, nc.gpsimd, nc.scalar, nc.scalar)):
+        for quad, queue in enumerate((nc.gpsimd, nc.scalar, nc.scalar, nc.scalar)):
             queue.dma_start(
                 w_scales[32 * quad : 32 * quad + 4, :, :].bitcast(I32),
                 w_scale_rows[4 * quad : 4 * quad + 4, :, :].bitcast(I32),
@@ -65,18 +66,18 @@ def tile_list_tabx_tm_none_kernel(tc, tab, w4_words, w4_scales, x, u, offs, out)
         u_raw = keep.tile([P, 4, M], F32, name="u_raw")
         nc.sync.dma_start(u_raw[:], u.rearrange("(p j) n -> p j n", j=4))
         tab_words.append(load_words(1))
+        w_codes = keep.tile([P, PASSES, 2 * M], U8, name="w_codes", align_bytes=64)
+        nc.sync.dma_start(w_codes[:].bitcast(I32), w4_words.rearrange("a p c -> p a c").bitcast(I32))
         tab_words.append(load_words(2))
 
         picked = keep.tile([P, S], U8, name="picked", align_bytes=64)
         nc.vector.tensor_copy(picked[:], window[:].bitcast(U8).indirect(offsets[:]))
-        for quad in range(4):
+        for quad in (0, 2, 1, 3):
             nc.sync.dma_start(
                 planes[32 * quad : 32 * quad + 4, :].bitcast(I32),
                 picked[16 * quad : 16 * quad + 16, :].bitcast(I32),
             )
 
-        w_codes = keep.tile([P, PASSES, 2 * M], U8, name="w_codes", align_bytes=64)
-        nc.sync.dma_start(w_codes[:].bitcast(I32), w4_words.rearrange("a p c -> p a c").bitcast(I32))
         x_first = load_x(0, 2 * P)
         x_raw = [x_first[:, :, 0:P], x_first[:, :, P : 2 * P], load_x(2 * P, 3 * P)[:], load_x(3 * P, 4 * P)[:]]
 
@@ -97,7 +98,7 @@ def tile_list_tabx_tm_none_kernel(tc, tab, w4_words, w4_scales, x, u, offs, out)
                 nc.tensor.matmul_mx(
                     out=acc[c][:],
                     lhsT=picked_words[a][:, c * P : (c + 1) * P].bitcast(E4M3),
-                    lhsT_scale=planes[:, a * S + c * P : a * S + (c + 1) * P],
+                    lhsT_scale=planes[:, SLOT_OF_PASS[a] * S + c * P : SLOT_OF_PASS[a] * S + (c + 1) * P],
                     rhs=w_codes[:, a, :].bitcast(E2M1),
                     rhs_scale=w_scales[:, a, :],
                     start=(a == 0),

@@ -130,6 +130,6 @@ def tile_list_tabx_tm_none_kernel(tc, tab, w4_words, w4_scales, x, u, offs, out)
                 start=False,
                 stop=True,
             )
-            result = keep.tile([P, M], F32, name="result%d" % c)
-            emptiers[c](result[:], acc[c][:])
-            nc.sync.dma_start(out[c * P : (c + 1) * P, :], result[:])
+            result = x_raw[2][:, c, :] if c < 3 else x_raw[3][:, 0, :]
+            emptiers[c](result, acc[c][:])
+            nc.sync.dma_start(out[c * P : (c + 1) * P, :], result)

@@ -39,8 +39,8 @@ def tile_list_tabx_tm_none_kernel(tc, tab, w4_words, w4_scales, x, u, offs, out)
         nc.vector.memset(planes[:].bitcast(I32), 0)
 
         scale_rows = tab[:, 512 * T :].rearrange("a (q t) -> a q t", t=T)
-        nc.sync.dma_start(window[0:64:2, :], scale_rows[0:2].rearrange("a q t -> q a t").bitcast(I32))
-        nc.sync.dma_start(window[1:64:4, :], scale_rows[2].bitcast(I32))
+        nc.sync.dma_start(window[32:96:2, :], scale_rows[0:2].rearrange("a q t -> q a t").bitcast(I32))
+        nc.sync.dma_start(window[33:96:4, :], scale_rows[2].bitcast(I32))
 
         w_scale_rows = w4_scales.rearrange("a q n -> q a n")
         for quad, queue in enumerate((nc.gpsimd, nc.scalar, nc.scalar, nc.scalar)):
@@ -75,14 +75,18 @@ def tile_list_tabx_tm_none_kernel(tc, tab, w4_words, w4_scales, x, u, offs, out)
         for quad in (0, 2, 1, 3):
             nc.sync.dma_start(
                 planes[32 * quad : 32 * quad + 4, :].bitcast(I32),
-                picked[16 * quad : 16 * quad + 16, :].bitcast(I32),
+                picked[32 + 16 * quad : 32 + 16 * quad + 16, :].bitcast(I32),
             )
 
         x_first = load_x(0, 2 * P)
         x_raw = [x_first[:, :, 0:P], x_first[:, :, P : 2 * P], load_x(2 * P, 3 * P)[:], load_x(3 * P, 4 * P)[:]]
 
         u_bf = keep.tile([P, M, 4], BF16, name="u_bf", align_bytes=64)
-        nc.scalar.copy(u_bf[:], u_raw[:].rearrange("p j n -> p n j"))
+
+        def interleave(copy, bf, raw):
+            copy(bf.rearrange("p (c i) j -> p c j i", i=4), raw.rearrange("p j (c i) -> p c j i", i=4))
+
+        interleave(nc.scalar.copy, u_bf[:], u_raw[:])
         u_codes = keep.tile([P, M], U32, name="u_codes", align_bytes=64)
         u_scales = keep.tile([P, M], U8, name="u_scales", align_bytes=64)
         x_codes = keep.tile([P, S], U32, name="x_codes", align_bytes=64)
@@ -115,7 +119,7 @@ def tile_list_tabx_tm_none_kernel(tc, tab, w4_words, w4_scales, x, u, offs, out)
         x_bf = []
         for c in range(TILES):
             x_bf.append(keep.tile([P, P, 4], BF16, name="x_bf%d" % c, align_bytes=64))
-            rounders[c](x_bf[c][:], x_raw[c].rearrange("p j s -> p s j"))
+            interleave(rounders[c], x_bf[c][:], x_raw[c])
         for c in range(TILES):
             cols = slice(c * P, (c + 1) * P)
             nc.vector.quantize_mx(

@@ -29,12 +29,12 @@ def tile_list_tabx_tm_none_kernel(tc, tab, w4_words, w4_scales, x, u, offs, out)
         nc.sync.dma_start(offsets[:], offs)
 
         window = keep.tile([P, T // 4], I32, name="window", align_bytes=64)
-        nc.gpsimd.memset(window[:], 0)
+        nc.vector.memset(window[:], 0)
         w_scales = keep.tile([P, PASSES, M], U8, name="w_scales", align_bytes=64)
-        nc.gpsimd.memset(w_scales[:].bitcast(I32), 0)
+        nc.vector.memset(w_scales[:].bitcast(I32), 0)
         warm = keep.tile([P, 1], F32, name="warm")
         warmed = keep.tile([P, 1], F32, name="warmed")
-        nc.gpsimd.memset(warm[:], 0.0)
+        nc.vector.memset(warm[:], 0.0)
         planes = keep.tile([P, SLOTS * S], U8, name="planes", align_bytes=64)
         nc.vector.memset(planes[:].bitcast(I32), 0)
 

@@ -27,14 +27,13 @@ def tile_list_tabx_tm_none_kernel(tc, tab, w4_words, w4_scales, x, u, offs, out)
     ):
         offsets = keep.tile([P, S // 16], U16, name="offsets")
         nc.sync.dma_start(offsets[:], offs)
+        u_raw = keep.tile([P, 4, M], F32, name="u_raw")
+        nc.sync.dma_start(u_raw[:], u.rearrange("(p j) n -> p j n", j=4))
 
         window = keep.tile([P, T // 4], I32, name="window", align_bytes=64)
         nc.vector.memset(window[:], 0)
         w_scales = keep.tile([P, PASSES, M], U8, name="w_scales", align_bytes=64)
         nc.vector.memset(w_scales[:].bitcast(I32), 0)
-        warm = keep.tile([P, 1], F32, name="warm")
-        warmed = keep.tile([P, 1], F32, name="warmed")
-        nc.vector.memset(warm[:], 0.0)
         planes = keep.tile([P, SLOTS * S], U8, name="planes", align_bytes=64)
         nc.vector.memset(planes[:].bitcast(I32), 0)
 
@@ -48,7 +47,6 @@ def tile_list_tabx_tm_none_kernel(tc, tab, w4_words, w4_scales, x, u, offs, out)
                 w_scales[32 * quad : 32 * quad + 4, :, :].bitcast(I32),
                 w_scale_rows[4 * quad : 4 * quad + 4, :, :].bitcast(I32),
             )
-        nc.scalar.copy(warmed[:], warm[:])
 
         def load_words(a):
             words = keep.tile([P, T], I32, name="tab_words%d" % a, align_bytes=64)
@@ -63,8 +61,6 @@ def tile_list_tabx_tm_none_kernel(tc, tab, w4_words, w4_scales, x, u, offs, out)
             return raw
 
         tab_words = [load_words(0)]
-        u_raw = keep.tile([P, 4, M], F32, name="u_raw")
-        nc.sync.dma_start(u_raw[:], u.rearrange("(p j) n -> p j n", j=4))
         tab_words.append(load_words(1))
         w_codes = keep.tile([P, PASSES, 2 * M], U8, name="w_codes", align_bytes=64)
         nc.sync.dma_start(w_codes[:].bitcast(I32), w4_words.rearrange("a p c -> p a c").bitcast(I32))

@@ -42,7 +42,7 @@ def tile_list_tabx_tm_none_kernel(tc, tab, w4_words, w4_scales, x, u, offs, out)
         nc.sync.dma_start(window[33:96:4, :], scale_rows[2].bitcast(I32))
 
         w_scale_rows = w4_scales.rearrange("a q n -> q a n")
-        for quad, queue in enumerate((nc.gpsimd, nc.scalar, nc.scalar, nc.scalar)):
+        for quad, queue in enumerate((nc.gpsimd, nc.scalar, nc.gpsimd, nc.scalar)):
             queue.dma_start(
                 w_scales[32 * quad : 32 * quad + 4, :, :].bitcast(I32),
                 w_scale_rows[4 * quad : 4 * quad + 4, :, :].bitcast(I32),

@@ -25,10 +25,10 @@ def tile_list_tabx_tm_none_kernel(tc, tab, w4_words, w4_scales, x, u, offs, out)
         tc.tile_pool(name="keep", bufs=1) as keep,
         tc.psum_pool(name="psum", bufs=1) as psum,
     ):
-        offsets = keep.tile([P, S // 16], U16, name="offsets")
-        nc.sync.dma_start(offsets[:], offs)
         u_raw = keep.tile([P, 4, M], F32, name="u_raw")
         nc.sync.dma_start(u_raw[:], u.rearrange("(p j) n -> p j n", j=4))
+        offsets = keep.tile([P, S // 16], U16, name="offsets")
+        nc.sync.dma_start(offsets[:], offs)
 
         window = keep.tile([P, T // 4], I32, name="window", align_bytes=64)
         nc.vector.memset(window[:], 0)

@@ -17,6 +17,7 @@ PASSES = K // 512
 SLOTS = 4
 SLOT_OF_PASS = (0, 2, 1)
 TILES = S // P
+SCALAR_SHARE = (88, 128, 48)
 
 
 def tile_list_tabx_tm_none_kernel(tc, tab, w4_words, w4_scales, x, u, offs, out):
@@ -75,7 +76,7 @@ def tile_list_tabx_tm_none_kernel(tc, tab, w4_words, w4_scales, x, u, offs, out)
             )
 
         x_first = load_x(0, 2 * P)
-        x_raw = [x_first[:, :, 0:P], x_first[:, :, P : 2 * P], load_x(2 * P, 3 * P)[:], load_x(3 * P, 4 * P)[:]]
+        x_raw = [x_first, load_x(2 * P, 3 * P), load_x(3 * P, 4 * P)]
 
         u_bf = keep.tile([P, M, 4], BF16, name="u_bf", align_bytes=64)
 
@@ -110,16 +111,21 @@ def tile_list_tabx_tm_none_kernel(tc, tab, w4_words, w4_scales, x, u, offs, out)
         table_pass(1)
         table_pass(2)
 
-        rounders = (nc.scalar.copy, nc.vector.tensor_copy, nc.scalar.copy, nc.vector.tensor_copy)
-        emptiers = (nc.scalar.copy, nc.scalar.copy, nc.scalar.copy, nc.vector.tensor_copy)
-        x_bf = []
-        for c in range(TILES):
-            x_bf.append(keep.tile([P, P, 4], BF16, name="x_bf%d" % c, align_bytes=64))
-            interleave(rounders[c], x_bf[c][:], x_raw[c])
-        for c in range(TILES):
+        rounded = [
+            keep.tile([P, raw.shape[2], 4], BF16, name="x_bf%d" % i, align_bytes=64) for i, raw in enumerate(x_raw)
+        ]
+        x_bf = [rounded[0][:, 0:P, :], rounded[0][:, P : 2 * P, :], rounded[1][:], rounded[2][:]]
+
+        def round_load(i):
+            share = SCALAR_SHARE[i]
+            if share < x_raw[i].shape[2]:
+                interleave(nc.vector.tensor_copy, rounded[i][:, share:, :], x_raw[i][:, :, share:])
+            interleave(nc.scalar.copy, rounded[i][:, 0:share, :], x_raw[i][:, :, 0:share])
+
+        def dense_pass(c):
             cols = slice(c * P, (c + 1) * P)
             nc.vector.quantize_mx(
-                x_codes[:, cols].bitcast(E4M3), x_scales[:, cols], x_bf[c][:].rearrange("p s j -> p (s j)")
+                x_codes[:, cols].bitcast(E4M3), x_scales[:, cols], x_bf[c].rearrange("p s j -> p (s j)")
             )
             nc.tensor.matmul_mx(
                 out=acc[c][:],
@@ -130,6 +136,17 @@ def tile_list_tabx_tm_none_kernel(tc, tab, w4_words, w4_scales, x, u, offs, out)
                 start=False,
                 stop=True,
             )
-            result = x_raw[2][:, c, :] if c < 3 else x_raw[3][:, 0, :]
+
+        round_load(0)
+        round_load(1)
+        dense_pass(0)
+        dense_pass(1)
+        round_load(2)
+        dense_pass(2)
+        dense_pass(3)
+
+        emptiers = (nc.scalar.copy, nc.scalar.copy, nc.scalar.copy, nc.vector.tensor_copy)
+        for c in range(TILES):
+            result = x_raw[2][:, c, :]
             emptiers[c](result, acc[c][:])
             nc.sync.dma_start(out[c * P : (c + 1) * P, :], result)

@@ -17,7 +17,7 @@ PASSES = K // 512
 SLOTS = 4
 SLOT_OF_PASS = (0, 2, 1)
 TILES = S // P
-SCALAR_SHARE = (88, 128, 48)
+SCALAR_SHARE = (88, 128, 64)
 
 
 def tile_list_tabx_tm_none_kernel(tc, tab, w4_words, w4_scales, x, u, offs, out):
@@ -122,11 +122,19 @@ def tile_list_tabx_tm_none_kernel(tc, tab, w4_words, w4_scales, x, u, offs, out)
                 interleave(nc.vector.tensor_copy, rounded[i][:, share:, :], x_raw[i][:, :, share:])
             interleave(nc.scalar.copy, rounded[i][:, 0:share, :], x_raw[i][:, :, 0:share])
 
+        def quantise(c, t0, t1):
+            cols = slice(c * P + t0, c * P + t1)
+            nc.vector.quantize_mx(
+                x_codes[:, cols].bitcast(E4M3), x_scales[:, cols], x_bf[c][:, t0:t1, :].rearrange("p s j -> p (s j)")
+            )
+
         def dense_pass(c):
             cols = slice(c * P, (c + 1) * P)
-            nc.vector.quantize_mx(
-                x_codes[:, cols].bitcast(E4M3), x_scales[:, cols], x_bf[c].rearrange("p s j -> p (s j)")
-            )
+            if c < TILES - 1:
+                quantise(c, 0, P)
+            else:
+                quantise(c, P // 2, P)
+                quantise(c, 0, P // 2)
             nc.tensor.matmul_mx(
                 out=acc[c][:],
                 lhsT=x_codes[:, cols].bitcast(E4M3),

@@ -63,9 +63,9 @@ def tile_list_tabx_tm_none_kernel(tc, tab, w4_words, w4_scales, x, u, offs, out)
 
         tab_words = [load_words(0)]
         tab_words.append(load_words(1))
+        tab_words.append(load_words(2))
         w_codes = keep.tile([P, PASSES, 2 * M], U8, name="w_codes", align_bytes=64)
         nc.sync.dma_start(w_codes[:].bitcast(I32), w4_words.rearrange("a p c -> p a c").bitcast(I32))
-        tab_words.append(load_words(2))
 
         picked = keep.tile([P, S], U8, name="picked", align_bytes=64)
         nc.vector.tensor_copy(picked[:], window[:].bitcast(U8).indirect(offsets[:]))

@@ -17,7 +17,8 @@ PASSES = K // 512
 SLOTS = 4
 SLOT_OF_PASS = (0, 2, 1)
 TILES = S // P
-SCALAR_SHARE = (88, 128, 64)
+X_CUTS = (0, 2 * P, 3 * P, 4 * P)
+SCALAR_SHARE = (100, 128, 40)
 
 
 def tile_list_tabx_tm_none_kernel(tc, tab, w4_words, w4_scales, x, u, offs, out):
@@ -75,8 +76,7 @@ def tile_list_tabx_tm_none_kernel(tc, tab, w4_words, w4_scales, x, u, offs, out)
                 picked[32 + 16 * quad : 32 + 16 * quad + 16, :].bitcast(I32),
             )
 
-        x_first = load_x(0, 2 * P)
-        x_raw = [x_first, load_x(2 * P, 3 * P), load_x(3 * P, 4 * P)]
+        x_raw = [load_x(c0, c1) for c0, c1 in zip(X_CUTS[:-1], X_CUTS[1:])]
 
         u_bf = keep.tile([P, M, 4], BF16, name="u_bf", align_bytes=64)
 
@@ -114,7 +114,6 @@ def tile_list_tabx_tm_none_kernel(tc, tab, w4_words, w4_scales, x, u, offs, out)
         rounded = [
             keep.tile([P, raw.shape[2], 4], BF16, name="x_bf%d" % i, align_bytes=64) for i, raw in enumerate(x_raw)
         ]
-        x_bf = [rounded[0][:, 0:P, :], rounded[0][:, P : 2 * P, :], rounded[1][:], rounded[2][:]]
 
         def round_load(i):
             share = SCALAR_SHARE[i]
@@ -122,19 +121,14 @@ def tile_list_tabx_tm_none_kernel(tc, tab, w4_words, w4_scales, x, u, offs, out)
                 interleave(nc.vector.tensor_copy, rounded[i][:, share:, :], x_raw[i][:, :, share:])
             interleave(nc.scalar.copy, rounded[i][:, 0:share, :], x_raw[i][:, :, 0:share])
 
-        def quantise(c, t0, t1):
-            cols = slice(c * P + t0, c * P + t1)
+        def quantise(i, t0, t1):
+            cols = slice(X_CUTS[i] + t0, X_CUTS[i] + t1)
             nc.vector.quantize_mx(
-                x_codes[:, cols].bitcast(E4M3), x_scales[:, cols], x_bf[c][:, t0:t1, :].rearrange("p s j -> p (s j)")
+                x_codes[:, cols].bitcast(E4M3), x_scales[:, cols], rounded[i][:, t0:t1, :].rearrange("p s j -> p (s j)")
             )
 
         def dense_pass(c):
             cols = slice(c * P, (c + 1) * P)
-            if c < TILES - 1:
-                quantise(c, 0, P)
-            else:
-                quantise(c, P // 2, P)
-                quantise(c, 0, P // 2)
             nc.tensor.matmul_mx(
                 out=acc[c][:],
                 lhsT=x_codes[:, cols].bitcast(E4M3),
@@ -147,13 +141,17 @@ def tile_list_tabx_tm_none_kernel(tc, tab, w4_words, w4_scales, x, u, offs, out)
 
         round_load(0)
         round_load(1)
+        quantise(0, 0, 2 * P)
         dense_pass(0)
         dense_pass(1)
         round_load(2)
+        quantise(1, 0, P)
         dense_pass(2)
+        quantise(2, P // 2, P)
+        quantise(2, 0, P // 2)
         dense_pass(3)
 
-        emptiers = (nc.scalar.copy, nc.scalar.copy, nc.scalar.copy, nc.vector.tensor_copy)
+        emptiers = (nc.scalar.copy, nc.scalar.copy, nc.vector.tensor_copy, nc.vector.tensor_copy)
         for c in range(TILES):
             result = x_raw[2][:, c, :]
             emptiers[c](result, acc[c][:])

@@ -27,16 +27,16 @@ def tile_list_tabx_tm_none_kernel(tc, tab, w4_words, w4_scales, x, u, offs, out)
         tc.tile_pool(name="keep", bufs=1) as keep,
         tc.psum_pool(name="psum", bufs=1) as psum,
     ):
-        u_raw = keep.tile([P, 4, M], F32, name="u_raw")
+        u_raw = keep.tile([P, 4, M], F32, name="u_raw", align_bytes=256)
         nc.sync.dma_start(u_raw[:], u.rearrange("(p j) n -> p j n", j=4))
-        offsets = keep.tile([P, S // 16], U16, name="offsets")
+        offsets = keep.tile([P, S // 16], U16, name="offsets", align_bytes=256)
         nc.sync.dma_start(offsets[:], offs)
 
-        window = keep.tile([P, T // 4], I32, name="window", align_bytes=64)
+        window = keep.tile([P, T // 4], I32, name="window", align_bytes=256)
         nc.vector.memset(window[:], 0)
-        w_scales = keep.tile([P, PASSES, M], U8, name="w_scales", align_bytes=64)
+        w_scales = keep.tile([P, PASSES, M], U8, name="w_scales", align_bytes=256)
         nc.vector.memset(w_scales[:].bitcast(I32), 0)
-        planes = keep.tile([P, SLOTS * S], U8, name="planes", align_bytes=64)
+        planes = keep.tile([P, SLOTS * S], U8, name="planes", align_bytes=256)
         nc.vector.memset(planes[:].bitcast(I32), 0)
 
         scale_rows = tab[:, 512 * T :].rearrange("a (q t) -> a q t", t=T)
@@ -51,24 +51,24 @@ def tile_list_tabx_tm_none_kernel(tc, tab, w4_words, w4_scales, x, u, offs, out)
             )
 
         def load_words(a):
-            words = keep.tile([P, T], I32, name="tab_words%d" % a, align_bytes=64)
+            words = keep.tile([P, T], I32, name="tab_words%d" % a, align_bytes=256)
             nc.sync.dma_start(words[:], tab[a, 0 : 512 * T].rearrange("(p c) -> p c", p=P).bitcast(I32))
             return words
 
         x_rows = x.rearrange("(p j) s -> p j s", j=4)
 
         def load_x(c0, c1):
-            raw = keep.tile([P, 4, c1 - c0], F32, name="x_raw%d" % c0)
+            raw = keep.tile([P, 4, c1 - c0], F32, name="x_raw%d" % c0, align_bytes=256)
             nc.sync.dma_start(raw[:], x_rows[:, :, c0:c1])
             return raw
 
         tab_words = [load_words(0)]
         tab_words.append(load_words(1))
         tab_words.append(load_words(2))
-        w_codes = keep.tile([P, PASSES, 2 * M], U8, name="w_codes", align_bytes=64)
+        w_codes = keep.tile([P, PASSES, 2 * M], U8, name="w_codes", align_bytes=256)
         nc.sync.dma_start(w_codes[:].bitcast(I32), w4_words.rearrange("a p c -> p a c").bitcast(I32))
 
-        picked = keep.tile([P, S], U8, name="picked", align_bytes=64)
+        picked = keep.tile([P, S], U8, name="picked", align_bytes=256)
         nc.vector.tensor_copy(picked[:], window[:].bitcast(U8).indirect(offsets[:]))
         for quad in (0, 2, 1, 3):
             nc.sync.dma_start(

@@ -14,11 +14,13 @@ E2M1 = mybir.dt.float4_e2m1fn_x4
 
 P = 128
 PASSES = K // 512
-SLOTS = 4
-SLOT_OF_PASS = (0, 2, 1)
 TILES = S // P
-X_CUTS = (0, 2 * P, 3 * P, 4 * P)
-SCALAR_SHARE = (100, 128, 40)
+LAST = PASSES - 1
+PAIR_ROW = 64
+LAST_ROW = 48
+LATE_TILES = (0, 1)
+EARLY_TILES = (2, 3)
+LAST_CUTS = (0, 2 * P, 3 * P, 4 * P)
 
 
 def tile_list_tabx_tm_none_kernel(tc, tab, w4_words, w4_scales, x, u, offs, out):
@@ -29,19 +31,22 @@ def tile_list_tabx_tm_none_kernel(tc, tab, w4_words, w4_scales, x, u, offs, out)
     ):
         u_raw = keep.tile([P, 4, M], F32, name="u_raw", align_bytes=256)
         nc.sync.dma_start(u_raw[:], u.rearrange("(p j) n -> p j n", j=4))
+
+        window = keep.tile([P, T // 4], I32, name="window", align_bytes=256)
+        scale_rows = tab[:, 512 * T :].rearrange("a (q t) -> a q t", t=T)
+        nc.sync.dma_start(window[PAIR_ROW : PAIR_ROW + 32, :], scale_rows[0:LAST].rearrange("a q t -> q a t").bitcast(I32))
+        nc.sync.dma_start(window[LAST_ROW : LAST_ROW + 16, :], scale_rows[LAST].bitcast(I32))
         offsets = keep.tile([P, S // 16], U16, name="offsets", align_bytes=256)
         nc.sync.dma_start(offsets[:], offs)
 
-        window = keep.tile([P, T // 4], I32, name="window", align_bytes=256)
-        nc.vector.memset(window[:], 0)
         w_scales = keep.tile([P, PASSES, M], U8, name="w_scales", align_bytes=256)
         nc.vector.memset(w_scales[:].bitcast(I32), 0)
-        planes = keep.tile([P, SLOTS * S], U8, name="planes", align_bytes=256)
-        nc.vector.memset(planes[:].bitcast(I32), 0)
-
-        scale_rows = tab[:, 512 * T :].rearrange("a (q t) -> a q t", t=T)
-        nc.sync.dma_start(window[32:96:2, :], scale_rows[0:2].rearrange("a q t -> q a t").bitcast(I32))
-        nc.sync.dma_start(window[33:96:4, :], scale_rows[2].bitcast(I32))
+        nc.vector.memset(window[0:LAST_ROW, :], 0)
+        nc.vector.memset(window[PAIR_ROW + 32 :, :], 0)
+        pair_planes = keep.tile([P, LAST * S], U8, name="pair_planes", align_bytes=256)
+        nc.vector.memset(pair_planes[:].bitcast(I32), 0)
+        last_plane = keep.tile([P, S], U8, name="last_plane", align_bytes=256)
+        nc.vector.memset(last_plane[:].bitcast(I32), 0)
 
         w_scale_rows = w4_scales.rearrange("a q n -> q a n")
         for quad, queue in enumerate((nc.gpsimd, nc.scalar, nc.gpsimd, nc.scalar)):
@@ -55,37 +60,35 @@ def tile_list_tabx_tm_none_kernel(tc, tab, w4_words, w4_scales, x, u, offs, out)
             nc.sync.dma_start(words[:], tab[a, 0 : 512 * T].rearrange("(p c) -> p c", p=P).bitcast(I32))
             return words
 
-        x_rows = x.rearrange("(p j) s -> p j s", j=4)
-
-        def load_x(c0, c1):
-            raw = keep.tile([P, 4, c1 - c0], F32, name="x_raw%d" % c0, align_bytes=256)
-            nc.sync.dma_start(raw[:], x_rows[:, :, c0:c1])
-            return raw
-
         tab_words = [load_words(0)]
+        x_raw = keep.tile([P, 4, S], F32, name="x_raw", align_bytes=256)
+        nc.sync.dma_start(x_raw[:], x.rearrange("(p j) s -> p j s", j=4))
         tab_words.append(load_words(1))
-        tab_words.append(load_words(2))
-        w_codes = keep.tile([P, PASSES, 2 * M], U8, name="w_codes", align_bytes=256)
-        nc.sync.dma_start(w_codes[:].bitcast(I32), w4_words.rearrange("a p c -> p a c").bitcast(I32))
 
         picked = keep.tile([P, S], U8, name="picked", align_bytes=256)
         nc.vector.tensor_copy(picked[:], window[:].bitcast(U8).indirect(offsets[:]))
         for quad in (0, 2, 1, 3):
             nc.sync.dma_start(
-                planes[32 * quad : 32 * quad + 4, :].bitcast(I32),
-                picked[32 + 16 * quad : 32 + 16 * quad + 16, :].bitcast(I32),
+                pair_planes[32 * quad : 32 * quad + 4, :].bitcast(I32),
+                picked[PAIR_ROW + 8 * quad : PAIR_ROW + 8 * quad + 8, :].bitcast(I32),
             )
-
-        x_raw = [load_x(c0, c1) for c0, c1 in zip(X_CUTS[:-1], X_CUTS[1:])]
-
-        u_bf = keep.tile([P, M, 4], BF16, name="u_bf", align_bytes=64)
+        w_codes = keep.tile([P, PASSES, 2 * M], U8, name="w_codes", align_bytes=256)
+        nc.sync.dma_start(w_codes[:].bitcast(I32), w4_words.rearrange("a p c -> p a c").bitcast(I32))
+        tab_words.append(load_words(2))
+        for quad in (0, 2, 1, 3):
+            nc.sync.dma_start(
+                last_plane[32 * quad : 32 * quad + 4, :].bitcast(I32),
+                picked[LAST_ROW + 4 * quad : LAST_ROW + 4 * quad + 4, :].bitcast(I32),
+            )
 
         def interleave(copy, bf, raw):
             copy(bf.rearrange("p (c i) j -> p c j i", i=4), raw.rearrange("p j (c i) -> p c j i", i=4))
 
+        u_bf = keep.tile([P, M, 4], BF16, name="u_bf", align_bytes=64)
         interleave(nc.scalar.copy, u_bf[:], u_raw[:])
         u_codes = keep.tile([P, M], U32, name="u_codes", align_bytes=64)
         u_scales = keep.tile([P, M], U8, name="u_scales", align_bytes=64)
+        x_bf = keep.tile([P, S, 4], BF16, name="x_bf", align_bytes=64)
         x_codes = keep.tile([P, S], U32, name="x_codes", align_bytes=64)
         x_scales = keep.tile([P, S], U8, name="x_scales", align_bytes=64)
         picked_words = [
@@ -93,38 +96,26 @@ def tile_list_tabx_tm_none_kernel(tc, tab, w4_words, w4_scales, x, u, offs, out)
         ]
         acc = [psum.tile([P, M], F32, name="acc%d" % c) for c in range(TILES)]
 
-        def table_pass(a):
-            nc.vector.tensor_copy(picked_words[a][:], tab_words[a][:].bitcast(U32).indirect(offsets[:]))
-            for c in range(TILES):
-                nc.tensor.matmul_mx(
-                    out=acc[c][:],
-                    lhsT=picked_words[a][:, c * P : (c + 1) * P].bitcast(E4M3),
-                    lhsT_scale=planes[:, SLOT_OF_PASS[a] * S + c * P : SLOT_OF_PASS[a] * S + (c + 1) * P],
-                    rhs=w_codes[:, a, :].bitcast(E2M1),
-                    rhs_scale=w_scales[:, a, :],
-                    start=(a == 0),
-                    stop=False,
-                )
+        def gather_words(a, t0, t1):
+            nc.vector.tensor_copy(
+                picked_words[a][:, t0:t1], tab_words[a][:].bitcast(U32).indirect(offsets[:, t0 // 16 : t1 // 16])
+            )
 
-        table_pass(0)
-        nc.vector.quantize_mx(u_codes[:].bitcast(E4M3), u_scales[:], u_bf[:].rearrange("p n j -> p (n j)"))
-        table_pass(1)
-        table_pass(2)
+        def table_pass(a, c):
+            plane = last_plane[:] if a == LAST else pair_planes[:, a * S : (a + 1) * S]
+            nc.tensor.matmul_mx(
+                out=acc[c][:],
+                lhsT=picked_words[a][:, c * P : (c + 1) * P].bitcast(E4M3),
+                lhsT_scale=plane[:, c * P : (c + 1) * P],
+                rhs=w_codes[:, a, :].bitcast(E2M1),
+                rhs_scale=w_scales[:, a, :],
+                start=(a == 0 and c in LATE_TILES),
+                stop=(a == LAST),
+            )
 
-        rounded = [
-            keep.tile([P, raw.shape[2], 4], BF16, name="x_bf%d" % i, align_bytes=64) for i, raw in enumerate(x_raw)
-        ]
-
-        def round_load(i):
-            share = SCALAR_SHARE[i]
-            if share < x_raw[i].shape[2]:
-                interleave(nc.vector.tensor_copy, rounded[i][:, share:, :], x_raw[i][:, :, share:])
-            interleave(nc.scalar.copy, rounded[i][:, 0:share, :], x_raw[i][:, :, 0:share])
-
-        def quantise(i, t0, t1):
-            cols = slice(X_CUTS[i] + t0, X_CUTS[i] + t1)
+        def quantise(t0, t1):
             nc.vector.quantize_mx(
-                x_codes[:, cols].bitcast(E4M3), x_scales[:, cols], rounded[i][:, t0:t1, :].rearrange("p s j -> p (s j)")
+                x_codes[:, t0:t1].bitcast(E4M3), x_scales[:, t0:t1], x_bf[:, t0:t1, :].rearrange("p s j -> p (s j)")
             )
 
         def dense_pass(c):
@@ -135,24 +126,36 @@ def tile_list_tabx_tm_none_kernel(tc, tab, w4_words, w4_scales, x, u, offs, out)
                 lhsT_scale=x_scales[:, cols],
                 rhs=u_codes[:].bitcast(E4M3),
                 rhs_scale=u_scales[:],
-                start=False,
-                stop=True,
+                start=(c in EARLY_TILES),
+                stop=False,
             )
 
-        round_load(0)
-        round_load(1)
-        quantise(0, 0, 2 * P)
-        dense_pass(0)
-        dense_pass(1)
-        round_load(2)
-        quantise(1, 0, P)
-        dense_pass(2)
-        quantise(2, P // 2, P)
-        quantise(2, 0, P // 2)
-        dense_pass(3)
+        gather_words(0, 0, S)
+        nc.vector.quantize_mx(u_codes[:].bitcast(E4M3), u_scales[:], u_bf[:].rearrange("p n j -> p (n j)"))
 
-        emptiers = (nc.scalar.copy, nc.scalar.copy, nc.vector.tensor_copy, nc.vector.tensor_copy)
+        half = S // 2
+        interleave(nc.scalar.copy, x_bf[:, half : 3 * P, :], x_raw[:, :, half : 3 * P])
+        interleave(nc.vector.tensor_copy, x_bf[:, 3 * P :, :], x_raw[:, :, 3 * P :])
+        interleave(nc.scalar.copy, x_bf[:, 0:half, :], x_raw[:, :, 0:half])
+        quantise(half, S)
+        for c in EARLY_TILES:
+            dense_pass(c)
         for c in range(TILES):
-            result = x_raw[2][:, c, :]
-            emptiers[c](result, acc[c][:])
-            nc.sync.dma_start(out[c * P : (c + 1) * P, :], result)
+            table_pass(0, c)
+
+        gather_words(1, 0, S)
+        for c in range(TILES):
+            table_pass(1, c)
+        quantise(0, half)
+        for c in LATE_TILES:
+            dense_pass(c)
+
+        result = keep.tile([P, TILES, M], F32, name="result", align_bytes=256)
+        for t0, t1 in zip(LAST_CUTS[:-1], LAST_CUTS[1:]):
+            gather_words(LAST, t0, t1)
+            for c in range(t0 // P, t1 // P):
+                table_pass(LAST, c)
+        for c in range(TILES):
+            empty = nc.vector.tensor_copy if c == TILES - 1 else nc.scalar.copy
+            empty(result[:, c, :], acc[c][:])
+            nc.sync.dma_start(out[c * P : (c + 1) * P, :], result[:, c, :])

@@ -18,9 +18,9 @@ TILES = S // P
 LAST = PASSES - 1
 PAIR_ROW = 64
 LAST_ROW = 48
-LATE_TILES = (0, 1)
-EARLY_TILES = (2, 3)
-LAST_CUTS = (0, 2 * P, 3 * P, 4 * P)
+X_CUTS = (0, 2 * P, 3 * P, 4 * P)
+EARLY_TILES = (0, 1)
+SCALAR_SHARE = (128, 128, 48)
 
 
 def tile_list_tabx_tm_none_kernel(tc, tab, w4_words, w4_scales, x, u, offs, out):
@@ -29,8 +29,8 @@ def tile_list_tabx_tm_none_kernel(tc, tab, w4_words, w4_scales, x, u, offs, out)
         tc.tile_pool(name="keep", bufs=1) as keep,
         tc.psum_pool(name="psum", bufs=1) as psum,
     ):
-        u_raw = keep.tile([P, 4, M], F32, name="u_raw", align_bytes=256)
-        nc.sync.dma_start(u_raw[:], u.rearrange("(p j) n -> p j n", j=4))
+        w_codes = keep.tile([P, PASSES, 2 * M], U8, name="w_codes", align_bytes=256)
+        nc.sync.dma_start(w_codes[:].bitcast(I32), w4_words.rearrange("a p c -> p a c").bitcast(I32))
 
         window = keep.tile([P, T // 4], I32, name="window", align_bytes=256)
         scale_rows = tab[:, 512 * T :].rearrange("a (q t) -> a q t", t=T)
@@ -60,32 +60,37 @@ def tile_list_tabx_tm_none_kernel(tc, tab, w4_words, w4_scales, x, u, offs, out)
             nc.sync.dma_start(words[:], tab[a, 0 : 512 * T].rearrange("(p c) -> p c", p=P).bitcast(I32))
             return words
 
-        tab_words = [load_words(0)]
-        x_raw = keep.tile([P, 4, S], F32, name="x_raw", align_bytes=256)
-        nc.sync.dma_start(x_raw[:], x.rearrange("(p j) s -> p j s", j=4))
-        tab_words.append(load_words(1))
+        x_rows = x.rearrange("(p j) s -> p j s", j=4)
+
+        def load_x(i):
+            c0, c1 = X_CUTS[i], X_CUTS[i + 1]
+            raw = keep.tile([P, 4, c1 - c0], F32, name="x_raw%d" % i, align_bytes=256)
+            nc.sync.dma_start(raw[:], x_rows[:, :, c0:c1])
+            return raw
 
         picked = keep.tile([P, S], U8, name="picked", align_bytes=256)
+
+        def move_scales(planes, first_row, passes):
+            for quad in (0, 2, 1, 3):
+                rows = slice(first_row + 4 * passes * quad, first_row + 4 * passes * (quad + 1))
+                nc.sync.dma_start(planes[32 * quad : 32 * quad + 4, :].bitcast(I32), picked[rows, :].bitcast(I32))
+
+        tab_words = [load_words(0)]
+        x_raw = [load_x(0)]
+        tab_words.append(load_words(1))
+        u_raw = keep.tile([P, 4, M], F32, name="u_raw", align_bytes=256)
+        nc.sync.dma_start(u_raw[:], u.rearrange("(p j) n -> p j n", j=4))
         nc.vector.tensor_copy(picked[:], window[:].bitcast(U8).indirect(offsets[:]))
-        for quad in (0, 2, 1, 3):
-            nc.sync.dma_start(
-                pair_planes[32 * quad : 32 * quad + 4, :].bitcast(I32),
-                picked[PAIR_ROW + 8 * quad : PAIR_ROW + 8 * quad + 8, :].bitcast(I32),
-            )
-        w_codes = keep.tile([P, PASSES, 2 * M], U8, name="w_codes", align_bytes=256)
-        nc.sync.dma_start(w_codes[:].bitcast(I32), w4_words.rearrange("a p c -> p a c").bitcast(I32))
+        move_scales(pair_planes, PAIR_ROW, LAST)
         tab_words.append(load_words(2))
-        for quad in (0, 2, 1, 3):
-            nc.sync.dma_start(
-                last_plane[32 * quad : 32 * quad + 4, :].bitcast(I32),
-                picked[LAST_ROW + 4 * quad : LAST_ROW + 4 * quad + 4, :].bitcast(I32),
-            )
+        x_raw.append(load_x(1))
+        x_raw.append(load_x(2))
+        move_scales(last_plane, LAST_ROW, 1)
 
         def interleave(copy, bf, raw):
             copy(bf.rearrange("p (c i) j -> p c j i", i=4), raw.rearrange("p j (c i) -> p c j i", i=4))
 
         u_bf = keep.tile([P, M, 4], BF16, name="u_bf", align_bytes=64)
-        interleave(nc.scalar.copy, u_bf[:], u_raw[:])
         u_codes = keep.tile([P, M], U32, name="u_codes", align_bytes=64)
         u_scales = keep.tile([P, M], U8, name="u_scales", align_bytes=64)
         x_bf = keep.tile([P, S, 4], BF16, name="x_bf", align_bytes=64)
@@ -109,8 +114,8 @@ def tile_list_tabx_tm_none_kernel(tc, tab, w4_words, w4_scales, x, u, offs, out)
                 lhsT_scale=plane[:, c * P : (c + 1) * P],
                 rhs=w_codes[:, a, :].bitcast(E2M1),
                 rhs_scale=w_scales[:, a, :],
-                start=(a == 0 and c in LATE_TILES),
-                stop=(a == LAST),
+                start=(a == 0),
+                stop=(a == LAST and c in EARLY_TILES),
             )
 
         def quantise(t0, t1):
@@ -126,36 +131,42 @@ def tile_list_tabx_tm_none_kernel(tc, tab, w4_words, w4_scales, x, u, offs, out)
                 lhsT_scale=x_scales[:, cols],
                 rhs=u_codes[:].bitcast(E4M3),
                 rhs_scale=u_scales[:],
-                start=(c in EARLY_TILES),
-                stop=False,
+                start=False,
+                stop=(c not in EARLY_TILES),
             )
 
-        gather_words(0, 0, S)
-        nc.vector.quantize_mx(u_codes[:].bitcast(E4M3), u_scales[:], u_bf[:].rearrange("p n j -> p (n j)"))
+        def round_load(i):
+            share, c0, c1 = SCALAR_SHARE[i], X_CUTS[i], X_CUTS[i + 1]
+            interleave(nc.scalar.copy, x_bf[:, c0 : c0 + share, :], x_raw[i][:, :, 0:share])
+            if c0 + share < c1:
+                interleave(nc.vector.tensor_copy, x_bf[:, c0 + share : c1, :], x_raw[i][:, :, share:])
 
-        half = S // 2
-        interleave(nc.scalar.copy, x_bf[:, half : 3 * P, :], x_raw[:, :, half : 3 * P])
-        interleave(nc.vector.tensor_copy, x_bf[:, 3 * P :, :], x_raw[:, :, 3 * P :])
-        interleave(nc.scalar.copy, x_bf[:, 0:half, :], x_raw[:, :, 0:half])
-        quantise(half, S)
-        for c in EARLY_TILES:
-            dense_pass(c)
+        gather_words(0, 0, S)
+        round_load(0)
+        quantise(0, 2 * P)
         for c in range(TILES):
             table_pass(0, c)
-
         gather_words(1, 0, S)
         for c in range(TILES):
             table_pass(1, c)
-        quantise(0, half)
-        for c in LATE_TILES:
-            dense_pass(c)
-
-        result = keep.tile([P, TILES, M], F32, name="result", align_bytes=256)
-        for t0, t1 in zip(LAST_CUTS[:-1], LAST_CUTS[1:]):
-            gather_words(LAST, t0, t1)
-            for c in range(t0 // P, t1 // P):
+        interleave(nc.scalar.copy, u_bf[:], u_raw[:])
+        nc.vector.quantize_mx(u_codes[:].bitcast(E4M3), u_scales[:], u_bf[:].rearrange("p n j -> p (n j)"))
+        dense_pass(0)
+        dense_pass(1)
+        for t0 in (0, S // 2):
+            gather_words(LAST, t0, t0 + S // 2)
+            for c in range(t0 // P, (t0 + S // 2) // P):
                 table_pass(LAST, c)
+        round_load(1)
+        round_load(2)
+        quantise(2 * P, 3 * P)
+        dense_pass(2)
+        quantise(3 * P + P // 2, S)
+        quantise(3 * P, 3 * P + P // 2)
+        dense_pass(3)
+
+        emptiers = (nc.scalar.copy, nc.scalar.copy, nc.vector.tensor_copy, nc.vector.tensor_copy)
         for c in range(TILES):
-            empty = nc.vector.tensor_copy if c == TILES - 1 else nc.scalar.copy
-            empty(result[:, c, :], acc[c][:])
-            nc.sync.dma_start(out[c * P : (c + 1) * P, :], result[:, c, :])
+            result = x_raw[2][:, c, :]
+            emptiers[c](result, acc[c][:])
+            nc.sync.dma_start(out[c * P : (c + 1) * P, :], result)

@@ -21,6 +21,7 @@ LAST_ROW = 48
 X_CUTS = (0, 2 * P, 3 * P, 4 * P)
 EARLY_TILES = (0, 1)
 SCALAR_SHARE = (128, 128, 48)
+STORES = ((0, 2), (2, 3), (3, 4))
 
 
 def tile_list_tabx_tm_none_kernel(tc, tab, w4_words, w4_scales, x, u, offs, out):
@@ -166,7 +167,8 @@ def tile_list_tabx_tm_none_kernel(tc, tab, w4_words, w4_scales, x, u, offs, out)
         dense_pass(3)
 
         emptiers = (nc.scalar.copy, nc.scalar.copy, nc.vector.tensor_copy, nc.vector.tensor_copy)
-        for c in range(TILES):
-            result = x_raw[2][:, c, :]
-            emptiers[c](result, acc[c][:])
-            nc.sync.dma_start(out[c * P : (c + 1) * P, :], result)
+        out_tiles = out.rearrange("(c p) n -> p c n", p=P)
+        for c0, c1 in STORES:
+            for c in range(c0, c1):
+                emptiers[c](x_raw[2][:, c, :], acc[c][:])
+            nc.sync.dma_start(out_tiles[:, c0:c1, :], x_raw[2][:, c0:c1, :])

@@ -21,7 +21,7 @@ LAST_ROW = 48
 X_CUTS = (0, 2 * P, 3 * P, 4 * P)
 EARLY_TILES = (0, 1)
 SCALAR_SHARE = (128, 128, 48)
-STORES = ((0, 2), (2, 3), (3, 4))
+STORES = ((0, 1), (1, 2), (2, 3), (3, 4))
 
 
 def tile_list_tabx_tm_none_kernel(tc, tab, w4_words, w4_scales, x, u, offs, out):
@@ -71,10 +71,10 @@ def tile_list_tabx_tm_none_kernel(tc, tab, w4_words, w4_scales, x, u, offs, out)
 
         picked = keep.tile([P, S], U8, name="picked", align_bytes=256)
 
-        def move_scales(planes, first_row, passes):
-            for quad in (0, 2, 1, 3):
+        def move_scales(queue, planes, first_row, passes, quads):
+            for quad in quads:
                 rows = slice(first_row + 4 * passes * quad, first_row + 4 * passes * (quad + 1))
-                nc.sync.dma_start(planes[32 * quad : 32 * quad + 4, :].bitcast(I32), picked[rows, :].bitcast(I32))
+                queue.dma_start(planes[32 * quad : 32 * quad + 4, :].bitcast(I32), picked[rows, :].bitcast(I32))
 
         tab_words = [load_words(0)]
         x_raw = [load_x(0)]
@@ -82,11 +82,12 @@ def tile_list_tabx_tm_none_kernel(tc, tab, w4_words, w4_scales, x, u, offs, out)
         u_raw = keep.tile([P, 4, M], F32, name="u_raw", align_bytes=256)
         nc.sync.dma_start(u_raw[:], u.rearrange("(p j) n -> p j n", j=4))
         nc.vector.tensor_copy(picked[:], window[:].bitcast(U8).indirect(offsets[:]))
-        move_scales(pair_planes, PAIR_ROW, LAST)
+        move_scales(nc.sync, pair_planes, PAIR_ROW, LAST, (0, 2, 1, 3))
+        move_scales(nc.gpsimd, last_plane, LAST_ROW, 1, (1,))
         tab_words.append(load_words(2))
         x_raw.append(load_x(1))
         x_raw.append(load_x(2))
-        move_scales(last_plane, LAST_ROW, 1)
+        move_scales(nc.sync, last_plane, LAST_ROW, 1, (2, 0, 3))
 
         def interleave(copy, bf, raw):
             copy(bf.rearrange("p (c i) j -> p c j i", i=4), raw.rearrange("p j (c i) -> p c j i", i=4))

@@ -83,11 +83,11 @@ def tile_list_tabx_tm_none_kernel(tc, tab, w4_words, w4_scales, x, u, offs, out)
         nc.sync.dma_start(u_raw[:], u.rearrange("(p j) n -> p j n", j=4))
         nc.vector.tensor_copy(picked[:], window[:].bitcast(U8).indirect(offsets[:]))
         move_scales(nc.sync, pair_planes, PAIR_ROW, LAST, (0, 2, 1, 3))
-        move_scales(nc.gpsimd, last_plane, LAST_ROW, 1, (1,))
+        move_scales(nc.gpsimd, last_plane, LAST_ROW, 1, (1, 3))
         tab_words.append(load_words(2))
         x_raw.append(load_x(1))
         x_raw.append(load_x(2))
-        move_scales(nc.sync, last_plane, LAST_ROW, 1, (2, 0, 3))
+        move_scales(nc.sync, last_plane, LAST_ROW, 1, (2, 0))
 
         def interleave(copy, bf, raw):
             copy(bf.rearrange("p (c i) j -> p c j i", i=4), raw.rearrange("p j (c i) -> p c j i", i=4))

import concourse.mybir as mybir

K, L, M, T, S = 1536, 512, 128, 1024, 512
FLOPS = 2 * S * M * (K + L)

F32 = mybir.dt.float32
BF16 = mybir.dt.bfloat16
I32 = mybir.dt.int32
U32 = mybir.dt.uint32
U16 = mybir.dt.uint16
U8 = mybir.dt.uint8
E4M3 = mybir.dt.float8_e4m3fn_x4
E2M1 = mybir.dt.float4_e2m1fn_x4

P = 128
PASSES = K // 512
TILES = S // P
LAST = PASSES - 1
PAIR_ROW = 64
LAST_ROW = 48
X_CUTS = (0, 2 * P, 3 * P, 4 * P)
EARLY_TILES = (0, 1)
SCALAR_SHARE = (128, 128, 48)
STORES = ((0, 1), (1, 2), (2, 3), (3, 4))


def tile_list_tabx_tm_none_kernel(tc, tab, w4_words, w4_scales, x, u, offs, out):
    nc = tc.nc
    with (
        tc.tile_pool(name="keep", bufs=1) as keep,
        tc.psum_pool(name="psum", bufs=1) as psum,
    ):
        w_codes = keep.tile([P, PASSES, 2 * M], U8, name="w_codes", align_bytes=256)
        nc.sync.dma_start(w_codes[:].bitcast(I32), w4_words.rearrange("a p c -> p a c").bitcast(I32))

        window = keep.tile([P, T // 4], I32, name="window", align_bytes=256)
        scale_rows = tab[:, 512 * T :].rearrange("a (q t) -> a q t", t=T)
        nc.sync.dma_start(window[PAIR_ROW : PAIR_ROW + 32, :], scale_rows[0:LAST].rearrange("a q t -> q a t").bitcast(I32))
        nc.sync.dma_start(window[LAST_ROW : LAST_ROW + 16, :], scale_rows[LAST].bitcast(I32))
        offsets = keep.tile([P, S // 16], U16, name="offsets", align_bytes=256)
        nc.sync.dma_start(offsets[:], offs)

        w_scales = keep.tile([P, PASSES, M], U8, name="w_scales", align_bytes=256)
        nc.vector.memset(w_scales[:].bitcast(I32), 0)
        nc.vector.memset(window[0:LAST_ROW, :], 0)
        nc.vector.memset(window[PAIR_ROW + 32 :, :], 0)
        pair_planes = keep.tile([P, LAST * S], U8, name="pair_planes", align_bytes=256)
        nc.vector.memset(pair_planes[:].bitcast(I32), 0)
        last_plane = keep.tile([P, S], U8, name="last_plane", align_bytes=256)
        nc.vector.memset(last_plane[:].bitcast(I32), 0)

        w_scale_rows = w4_scales.rearrange("a q n -> q a n")
        for quad, queue in enumerate((nc.gpsimd, nc.scalar, nc.gpsimd, nc.scalar)):
            queue.dma_start(
                w_scales[32 * quad : 32 * quad + 4, :, :].bitcast(I32),
                w_scale_rows[4 * quad : 4 * quad + 4, :, :].bitcast(I32),
            )

        def load_words(a):
            words = keep.tile([P, T], I32, name="tab_words%d" % a, align_bytes=256)
            nc.sync.dma_start(words[:], tab[a, 0 : 512 * T].rearrange("(p c) -> p c", p=P).bitcast(I32))
            return words

        x_rows = x.rearrange("(p j) s -> p j s", j=4)

        def load_x(i):
            c0, c1 = X_CUTS[i], X_CUTS[i + 1]
            raw = keep.tile([P, 4, c1 - c0], F32, name="x_raw%d" % i, align_bytes=256)
            nc.sync.dma_start(raw[:], x_rows[:, :, c0:c1])
            return raw

        picked = keep.tile([P, S], U8, name="picked", align_bytes=256)

        def move_scales(queue, planes, first_row, passes, quads):
            for quad in quads:
                rows = slice(first_row + 4 * passes * quad, first_row + 4 * passes * (quad + 1))
                queue.dma_start(planes[32 * quad : 32 * quad + 4, :].bitcast(I32), picked[rows, :].bitcast(I32))

        tab_words = [load_words(0)]
        x_raw = [load_x(0)]
        tab_words.append(load_words(1))
        u_raw = keep.tile([P, 4, M], F32, name="u_raw", align_bytes=256)
        nc.sync.dma_start(u_raw[:], u.rearrange("(p j) n -> p j n", j=4))
        nc.vector.tensor_copy(picked[:], window[:].bitcast(U8).indirect(offsets[:]))
        move_scales(nc.sync, pair_planes, PAIR_ROW, LAST, (0, 2, 1, 3))
        move_scales(nc.gpsimd, last_plane, LAST_ROW, 1, (1, 3))
        tab_words.append(load_words(2))
        x_raw.append(load_x(1))
        x_raw.append(load_x(2))
        move_scales(nc.sync, last_plane, LAST_ROW, 1, (2, 0))

        def interleave(copy, bf, raw):
            copy(bf.rearrange("p (c i) j -> p c j i", i=4), raw.rearrange("p j (c i) -> p c j i", i=4))

        u_bf = keep.tile([P, M, 4], BF16, name="u_bf", align_bytes=64)
        u_codes = keep.tile([P, M], U32, name="u_codes", align_bytes=64)
        u_scales = keep.tile([P, M], U8, name="u_scales", align_bytes=64)
        x_bf = keep.tile([P, S, 4], BF16, name="x_bf", align_bytes=64)
        x_codes = keep.tile([P, S], U32, name="x_codes", align_bytes=64)
        x_scales = keep.tile([P, S], U8, name="x_scales", align_bytes=64)
        picked_words = [
            keep.tile([P, S], U32, name="picked_words%d" % a, align_bytes=64) for a in range(PASSES)
        ]
        acc = [psum.tile([P, M], F32, name="acc%d" % c) for c in range(TILES)]

        def gather_words(a, t0, t1):
            nc.vector.tensor_copy(
                picked_words[a][:, t0:t1], tab_words[a][:].bitcast(U32).indirect(offsets[:, t0 // 16 : t1 // 16])
            )

        def table_pass(a, c):
            plane = last_plane[:] if a == LAST else pair_planes[:, a * S : (a + 1) * S]
            nc.tensor.matmul_mx(
                out=acc[c][:],
                lhsT=picked_words[a][:, c * P : (c + 1) * P].bitcast(E4M3),
                lhsT_scale=plane[:, c * P : (c + 1) * P],
                rhs=w_codes[:, a, :].bitcast(E2M1),
                rhs_scale=w_scales[:, a, :],
                start=(a == 0),
                stop=(a == LAST and c in EARLY_TILES),
            )

        def quantise(t0, t1):
            nc.vector.quantize_mx(
                x_codes[:, t0:t1].bitcast(E4M3), x_scales[:, t0:t1], x_bf[:, t0:t1, :].rearrange("p s j -> p (s j)")
            )

        def dense_pass(c):
            cols = slice(c * P, (c + 1) * P)
            nc.tensor.matmul_mx(
                out=acc[c][:],
                lhsT=x_codes[:, cols].bitcast(E4M3),
                lhsT_scale=x_scales[:, cols],
                rhs=u_codes[:].bitcast(E4M3),
                rhs_scale=u_scales[:],
                start=False,
                stop=(c not in EARLY_TILES),
            )

        def round_load(i):
            share, c0, c1 = SCALAR_SHARE[i], X_CUTS[i], X_CUTS[i + 1]
            interleave(nc.scalar.copy, x_bf[:, c0 : c0 + share, :], x_raw[i][:, :, 0:share])
            if c0 + share < c1:
                interleave(nc.vector.tensor_copy, x_bf[:, c0 + share : c1, :], x_raw[i][:, :, share:])

        gather_words(0, 0, S)
        round_load(0)
        quantise(0, 2 * P)
        for c in range(TILES):
            table_pass(0, c)
        gather_words(1, 0, S)
        for c in range(TILES):
            table_pass(1, c)
        interleave(nc.scalar.copy, u_bf[:], u_raw[:])
        nc.vector.quantize_mx(u_codes[:].bitcast(E4M3), u_scales[:], u_bf[:].rearrange("p n j -> p (n j)"))
        dense_pass(0)
        dense_pass(1)
        for t0 in (0, S // 2):
            gather_words(LAST, t0, t0 + S // 2)
            for c in range(t0 // P, (t0 + S // 2) // P):
                table_pass(LAST, c)
        round_load(1)
        round_load(2)
        quantise(2 * P, 3 * P)
        dense_pass(2)
        quantise(3 * P + P // 2, S)
        quantise(3 * P, 3 * P + P // 2)
        dense_pass(3)

        emptiers = (nc.scalar.copy, nc.scalar.copy, nc.vector.tensor_copy, nc.vector.tensor_copy)
        out_tiles = out.rearrange("(c p) n -> p c n", p=P)
        for c0, c1 in STORES:
            for c in range(c0, c1):
                emptiers[c](x_raw[2][:, c, :], acc[c][:])
            nc.sync.dma_start(out_tiles[:, c0:c1, :], x_raw[2][:, c0:c1, :])
